import numpy as np
import ml_dtypes


def mxq(x, axis, fmt="e4m3"):
    dtype, down = {"e4m3": (ml_dtypes.float8_e4m3fn, 7), "e5m2": (ml_dtypes.float8_e5m2, 14)}[fmt]
    v = np.moveaxis(np.asarray(x, np.float32).astype(ml_dtypes.bfloat16).astype(np.float64), axis, -1)
    blocks = v.reshape(v.shape[:-1] + (-1, 32))
    amax = np.abs(blocks).max(-1, keepdims=True)
    byte = np.maximum(np.where(amax > 0, np.frexp(amax)[1] - 1 + 127, 0) - down, 1)
    scale = np.exp2(byte - 127.0)
    codes = (blocks / scale).astype(np.float32).astype(dtype).astype(np.float64)
    return np.moveaxis((codes * scale).reshape(v.shape), -1, axis)


WIDE = False


def mx_kscale(k):
    if not WIDE:
        return np.ones(k)
    levels = np.array([10, -10, 5, -5, 0])
    if k % 512:
        return np.exp2(np.random.permutation(np.resize(levels, k // 32))).repeat(32)
    a = np.empty((k // 512, 16))
    for p in range(k // 512):
        a[p, :8] = np.random.permutation(np.resize(levels, 8))
        for g in range(8):
            far = levels[np.abs(levels - a[p, g]) >= 10]
            a[p, g + 8] = far[np.random.randint(len(far))]
    return np.exp2(a.ravel()).repeat(32)


def f64(x):
    return np.asarray(x).astype(np.float64)


def striped(idx):
    return np.tile(idx.reshape(-1, 16).T, (8, 1)).astype(np.uint16)


def unstriped(offs):
    return offs[:16].T.reshape(-1).astype(np.int64)


E2M1 = np.array([0.0, 0.5, 1.0, 1.5, 2.0, 3.0, 4.0, 6.0, -0.0, -0.5, -1.0, -1.5, -2.0, -3.0, -4.0, -6.0])


def pack_weight(w, fmt):
    k, n = w.shape
    w = f64(np.asarray(w, np.float32).astype(ml_dtypes.bfloat16)).reshape(k // 32, 32, n)
    amax = np.abs(w).max(1)
    if fmt == "e4m3":
        byte = np.frexp(amax)[1] - 1 + 127 - 7
    else:
        mant, ex = np.frexp(amax / 6.0)
        byte = np.where(mant > 0.5, ex, ex - 1) + 127
    byte = np.clip(np.where(amax > 0, byte, 1), 1, 254)
    scaled = (w * np.exp2(127.0 - byte)[:, None, :]).reshape(k, n).astype(np.float32)
    by_word = np.ascontiguousarray(scaled.reshape(k // 512, 128, 4, n).transpose(0, 1, 3, 2))
    if fmt == "e4m3":
        words = by_word.astype(ml_dtypes.float8_e4m3fn).view(np.uint8)
    else:
        c = by_word.astype(ml_dtypes.float4_e2m1fn).view(np.uint8) & 0xF
        words = (c[..., 0::2] | (c[..., 1::2] << 4)).reshape(k // 512, 128, 2 * n)
    return np.ascontiguousarray(words), np.ascontiguousarray(byte.astype(np.uint8).reshape(k // 512, 16, n))


def unpack_weight(words, scales, fmt):
    g, _, n = scales.shape
    words = np.ascontiguousarray(words).reshape(g, 128, n, -1)
    if fmt == "e4m3":
        vals = words.view(ml_dtypes.float8_e4m3fn).astype(np.float64)
    else:
        nib = np.empty((g, 128, n, 4), np.uint8)
        nib[..., 0::2] = words & 0xF
        nib[..., 1::2] = words >> 4
        vals = E2M1[nib]
    vals = vals * np.repeat(np.exp2(scales.astype(np.float64) - 127.0), 8, axis=1)[..., None]
    return vals.transpose(0, 1, 3, 2).reshape(g * 512, n)


def pack_table(v):
    words, scales = pack_weight(v, "e4m3")
    return np.concatenate([words.reshape(words.shape[0], -1), scales.reshape(scales.shape[0], -1)], axis=1)


def unpack_table(tab):
    g, t = tab.shape[0], tab.shape[1] // 528
    return unpack_weight(tab[:, :512 * t].reshape(g, 128, t, 4), tab[:, 512 * t:].reshape(g, 16, t), "e4m3")


def gelu(v):
    return 0.5 * v * (1.0 + np.tanh(np.sqrt(2.0 / np.pi) * (v + 0.044715 * v**3)))


K, M, T, S = 2048, 512, 1024, 512


def setup_inputs():
    n = np.random.standard_normal
    s = mx_kscale(K)[:, None]
    return {
        "tab": pack_table(n((K, T)) * s),
        "w": (n((K, M)) / np.sqrt(K) / s).astype(np.float32),
        "b": (0.3 * n(512)).astype(np.float32),
        "wgo": np.tile(np.random.uniform(0.5, 2.0, S), (128, 1)).astype(np.float32),
        "offs": striped(np.random.permutation(T)[:S]),
        "offs2": striped(np.random.permutation(T)[:S]),
    }


def reference(tab, w, b, wgo, offs, offs2):
    tab_ = unpack_table(tab)[:, unstriped(offs)]
    w_ = mxq(f64(w), 0, "e4m3")
    y = w_.T @ tab_
    out = np.zeros((M, T))
    out[:, unstriped(offs2)] = f64(wgo)[0] * (gelu(y + f64(b)[:, None]))
    return out

@@ -1,0 +1,182 @@
+from contextlib import ExitStack
+
+import concourse.mybir as mybir
+
+F32 = mybir.dt.float32
+BF16 = mybir.dt.bfloat16
+I32 = mybir.dt.int32
+U32 = mybir.dt.uint32
+U16 = mybir.dt.uint16
+U8 = mybir.dt.uint8
+FP8X4 = mybir.dt.float8_e4m3fn_x4
+MULT = mybir.AluOpType.mult
+GELU = mybir.ActivationFunctionType.Gelu_apprx_tanh
+
+K, M, T, S = 2048, 512, 1024, 512
+P = 128
+PASSES = K // 512
+FLOPS = 2 * K * M * S
+BYTES = 528 * S * PASSES + 4 * K * M + 4 * M + 4 * S + 4 * P * S // 16 + 4 * M * T
+
+GROUPS = ((0, 128), (128, 256), (256, 512))
+HALF = S // 2
+
+
+def tile_list_tabscat_gelu_kernel(tc, tab, w, b, wgo, offs, offs2, out):
+    nc = tc.nc
+    with ExitStack() as ctx:
+        keep = ctx.enter_context(tc.tile_pool(name="keep", bufs=1))
+        psum = ctx.enter_context(tc.psum_pool(name="psum", bufs=1))
+
+        offs_t = keep.tile([P, S // 16], U16, name="offs_t")
+        offs2_t = keep.tile([P, S // 16], U16, name="offs2_t")
+        tab32 = tab.bitcast(I32)
+
+        planes = keep.tile([P, T], U8, name="planes", align_bytes=64)
+        nc.vector.memset(planes[:].bitcast(I32), 0)
+        wins = []
+        for m in range(4):
+            win = keep.tile([P, T], F32, name=f"win{m}")
+            wins.append(win)
+        nc.vector.memset(wins[0][:], 0.0)
+        nc.vector.memset(wins[1][:], 0.0)
+        nc.gpsimd.memset(wins[2][:], 0.0)
+        nc.gpsimd.memset(wins[3][:], 0.0)
+        warm = keep.tile([P, 1], F32, name="warm")
+        warm2 = keep.tile([P, 1], F32, name="warm2")
+        nc.gpsimd.memset(warm[:], 0.0)
+        nc.scalar.activation(warm2[:], warm[:], GELU)
+
+        words = []
+        raws = {}
+        for a in range(PASSES):
+            tw = keep.tile([P, T], I32, name=f"tab{a}", align_bytes=64)
+            words.append(tw)
+            for g, (c0, c1) in enumerate(GROUPS):
+                rw = keep.tile([P, 4, c1 - c0], F32, name=f"raw{a}_{g}")
+                raws[(a, g)] = rw
+
+        def load_tab(a):
+            nc.sync.dma_start(out=words[a][:], in_=tab32[a, 0 : P * T].rearrange("(p t) -> p t", t=T))
+
+        def load_w(a, g):
+            c0, c1 = GROUPS[g]
+            nc.sync.dma_start(out=raws[(a, g)][:], in_=w[512 * a : 512 * (a + 1), c0:c1].rearrange("(p j) c -> p j c", j=4))
+
+        nc.sync.dma_start(offs_t[:], offs)
+        for q in range(4):
+            nc.sync.dma_start(
+                out=planes[32 * q : 32 * q + 16, :].bitcast(I32),
+                in_=tab32[:, P * T + T * q : P * T + T * (q + 1)].rearrange("a (r t) -> a r t", r=4),
+            )
+        bias = keep.tile([P, 4], F32, name="bias")
+        nc.scalar.dma_start(out=bias[:], in_=b.rearrange("(m p) -> p m", p=P))
+        wgo_t = keep.tile([P, S], F32, name="wgo_t")
+        for a in range(PASSES):
+            load_tab(a)
+            load_w(a, 0)
+        nc.sync.dma_start(offs2_t[:], offs2)
+        nc.sync.dma_start(out=wgo_t[:], in_=wgo)
+        for g in range(1, len(GROUPS)):
+            for a in range(PASSES):
+                load_w(a, g)
+
+        gscales = keep.tile([P, S], U8, name="gscales", align_bytes=64)
+        nc.vector.tensor_copy(gscales[:], planes[:].indirect(offs_t[:]))
+        gwords = []
+        for a in range(PASSES):
+            gw = keep.tile([P, S], U32, name=f"gw{a}", align_bytes=64)
+            gwords.append(gw)
+        accs = []
+        for m in range(4):
+            acc = psum.tile([P, S], F32, name=f"acc{m}")
+            accs.append(acc)
+
+        codes = {}
+        scales = {}
+
+        groupeds = {}
+
+        def interleave(a, g):
+            c0, c1 = GROUPS[g]
+            width = c1 - c0
+            grouped = keep.tile([P, width, 4], BF16, name=f"grp{a}_{g}", align_bytes=64)
+            nc.scalar.copy(
+                out=grouped[:].rearrange("p (c i) j -> p c j i", i=4),
+                in_=raws[(a, g)][:].rearrange("p j (c i) -> p c j i", i=4),
+            )
+            groupeds[(a, g)] = grouped
+
+        def quantise(a, g):
+            c0, c1 = GROUPS[g]
+            width = c1 - c0
+            grouped = groupeds[(a, g)]
+            cd = keep.tile([P, width], U32, name=f"cd{a}_{g}", align_bytes=64)
+            sc = keep.tile([P, width], U8, name=f"sc{a}_{g}", align_bytes=64)
+            nc.vector.quantize_mx(out=cd[:].bitcast(FP8X4), scales=sc[:], in_=grouped[:].rearrange("p c j -> p (c j)"))
+            codes[(a, g)] = cd
+            scales[(a, g)] = sc
+
+        def multiply(a, g):
+            c0, c1 = GROUPS[g]
+            for m in range(c0 // P, c1 // P):
+                cols = slice(m * P - c0, (m + 1) * P - c0)
+                nc.tensor.matmul_mx(
+                    out=accs[m][:],
+                    lhsT=codes[(a, g)][:, cols].bitcast(FP8X4),
+                    lhsT_scale=scales[(a, g)][:, cols],
+                    rhs=gwords[a][:].bitcast(FP8X4),
+                    rhs_scale=gscales[4 * a : P, :],
+                    start=(a == 0),
+                    stop=(a == PASSES - 1),
+                )
+
+        acts = []
+        for m in range(4):
+            act = keep.tile([P, S], F32, name=f"act{m}")
+            acts.append(act)
+
+        def gelu(m):
+            nc.scalar.activation(acts[m][:], accs[m][:], GELU, bias=bias[:, m : m + 1])
+
+        def scatter(m, h):
+            cols = slice(h * HALF, (h + 1) * HALF)
+            ocols = slice(h * HALF // 16, (h + 1) * HALF // 16)
+            nc.vector.tensor_tensor(wins[m][:].indirect(offs2_t[:, ocols]), acts[m][:, cols], wgo_t[:, cols], MULT)
+
+        def store(m):
+            nc.sync.dma_start(out=out[m * P : (m + 1) * P, :], in_=wins[m][:])
+
+        for a in range(PASSES):
+            nc.vector.tensor_copy(gwords[a][:], words[a][:].bitcast(U32).indirect(offs_t[:]))
+            interleave(a, 0)
+            quantise(a, 0)
+            multiply(a, 0)
+        interleave(0, 1)
+        interleave(1, 1)
+        gelu(0)
+        interleave(2, 1)
+        interleave(3, 1)
+        scatter(0, 0)
+        for a in range(PASSES):
+            quantise(a, 1)
+            multiply(a, 1)
+        interleave(0, 2)
+        interleave(1, 2)
+        gelu(1)
+        interleave(2, 2)
+        interleave(3, 2)
+        scatter(0, 1)
+        store(0)
+        scatter(1, 0)
+        for a in range(PASSES):
+            quantise(a, 2)
+            multiply(a, 2)
+        gelu(2)
+        gelu(3)
+        scatter(1, 1)
+        store(1)
+        for m in (2, 3):
+            scatter(m, 0)
+            scatter(m, 1)
+            store(m)

@@ -72,9 +72,14 @@ def tile_list_tabscat_gelu_kernel(tc, tab, w, b, wgo, offs, offs2, out):
         bias = keep.tile([P, 4], F32, name="bias")
         nc.scalar.dma_start(out=bias[:], in_=b.rearrange("(m p) -> p m", p=P))
         wgo_t = keep.tile([P, S], F32, name="wgo_t")
-        for a in range(PASSES):
-            load_tab(a)
-            load_w(a, 0)
+        load_tab(0)
+        load_w(0, 0)
+        load_tab(1)
+        load_w(1, 0)
+        load_tab(2)
+        load_w(2, 0)
+        load_w(3, 0)
+        load_tab(3)
         nc.sync.dma_start(offs2_t[:], offs2)
         nc.sync.dma_start(out=wgo_t[:], in_=wgo)
         for g in range(1, len(GROUPS)):
@@ -87,96 +92,88 @@ def tile_list_tabscat_gelu_kernel(tc, tab, w, b, wgo, offs, offs2, out):
         for a in range(PASSES):
             gw = keep.tile([P, S], U32, name=f"gw{a}", align_bytes=64)
             gwords.append(gw)
+
         accs = []
         for m in range(4):
-            acc = psum.tile([P, S], F32, name=f"acc{m}")
-            accs.append(acc)
+            row = []
+            for h in range(2 if m == 0 else 1):
+                acc = psum.tile([P, HALF if m == 0 else S], F32, name=f"acc{m}_{h}")
+                row.append(acc)
+            accs.append(row)
 
         codes = {}
         scales = {}
 
-        groupeds = {}
-
-        def interleave(a, g):
+        def quantise(a, g):
             c0, c1 = GROUPS[g]
             width = c1 - c0
-            grouped = keep.tile([P, width, 4], BF16, name=f"grp{a}_{g}", align_bytes=64)
+            grouped = keep.tile([P, width, 4], BF16, name=f"grp{a}_{g}", tag=f"grp{a}_{g}", align_bytes=64)
             nc.scalar.copy(
                 out=grouped[:].rearrange("p (c i) j -> p c j i", i=4),
                 in_=raws[(a, g)][:].rearrange("p j (c i) -> p c j i", i=4),
             )
-            groupeds[(a, g)] = grouped
-
-        def quantise(a, g):
-            c0, c1 = GROUPS[g]
-            width = c1 - c0
-            grouped = groupeds[(a, g)]
             cd = keep.tile([P, width], U32, name=f"cd{a}_{g}", align_bytes=64)
             sc = keep.tile([P, width], U8, name=f"sc{a}_{g}", align_bytes=64)
             nc.vector.quantize_mx(out=cd[:].bitcast(FP8X4), scales=sc[:], in_=grouped[:].rearrange("p c j -> p (c j)"))
             codes[(a, g)] = cd
             scales[(a, g)] = sc
 
-        def multiply(a, g):
+        def gather(a, h0, h1):
+            nc.vector.tensor_copy(gwords[a][:, h0:h1], words[a][:].bitcast(U32).indirect(offs_t[:, h0 // 16 : h1 // 16]))
+
+        def multiply(a, g, h):
             c0, c1 = GROUPS[g]
             for m in range(c0 // P, c1 // P):
                 cols = slice(m * P - c0, (m + 1) * P - c0)
+                toks = slice(h * HALF, (h + 1) * HALF) if m == 0 else slice(0, S)
                 nc.tensor.matmul_mx(
-                    out=accs[m][:],
+                    out=accs[m][h][:],
                     lhsT=codes[(a, g)][:, cols].bitcast(FP8X4),
                     lhsT_scale=scales[(a, g)][:, cols],
-                    rhs=gwords[a][:].bitcast(FP8X4),
-                    rhs_scale=gscales[4 * a : P, :],
+                    rhs=gwords[a][:, toks].bitcast(FP8X4),
+                    rhs_scale=gscales[4 * a : P, toks],
                     start=(a == 0),
                     stop=(a == PASSES - 1),
                 )
 
-        acts = []
-        for m in range(4):
-            act = keep.tile([P, S], F32, name=f"act{m}")
-            acts.append(act)
+        acts = {}
 
-        def gelu(m):
-            nc.scalar.activation(acts[m][:], accs[m][:], GELU, bias=bias[:, m : m + 1])
+        def gelu(m, h):
+            tag = ("grp2_1", "grp2_2", "act2_1", "act3_1")[m] if h else f"act{m}_0"
+            act = keep.tile([P, HALF], F32, name=f"act{m}_{h}", tag=tag, align_bytes=64)
+            acc = accs[0][h][:] if m == 0 else accs[m][0][:, h * HALF : (h + 1) * HALF]
+            nc.scalar.activation(act[:], acc, GELU, bias=bias[:, m : m + 1])
+            acts[(m, h)] = act
 
         def scatter(m, h):
             cols = slice(h * HALF, (h + 1) * HALF)
             ocols = slice(h * HALF // 16, (h + 1) * HALF // 16)
-            nc.vector.tensor_tensor(wins[m][:].indirect(offs2_t[:, ocols]), acts[m][:, cols], wgo_t[:, cols], MULT)
+            nc.vector.tensor_tensor(wins[m][:].indirect(offs2_t[:, ocols]), acts[(m, h)][:], wgo_t[:, cols], MULT)
 
         def store(m):
             nc.sync.dma_start(out=out[m * P : (m + 1) * P, :], in_=wins[m][:])
 
         for a in range(PASSES):
-            nc.vector.tensor_copy(gwords[a][:], words[a][:].bitcast(U32).indirect(offs_t[:]))
-            interleave(a, 0)
             quantise(a, 0)
-            multiply(a, 0)
-        interleave(0, 1)
-        interleave(1, 1)
-        gelu(0)
-        interleave(2, 1)
-        interleave(3, 1)
-        scatter(0, 0)
-        for a in range(PASSES):
-            quantise(a, 1)
-            multiply(a, 1)
-        interleave(0, 2)
-        interleave(1, 2)
-        gelu(1)
-        interleave(2, 2)
-        interleave(3, 2)
-        scatter(0, 1)
-        store(0)
-        scatter(1, 0)
-        for a in range(PASSES):
-            quantise(a, 2)
-            multiply(a, 2)
-        gelu(2)
-        gelu(3)
-        scatter(1, 1)
-        store(1)
-        for m in (2, 3):
+            if a < PASSES - 1:
+                gather(a, 0, S)
+            else:
+                gather(a, 0, HALF)
+                gather(a, HALF, S)
+            multiply(a, 0, 0)
+            multiply(a, 0, 1)
+        gelu(0, 0)
+        for g in range(1, len(GROUPS)):
+            for a in range(PASSES):
+                quantise(a, g)
+                multiply(a, g, 0)
+                if a == 2:
+                    gelu(g - 1, 1)
+            gelu(g, 0)
+        gelu(2, 1)
+        gelu(3, 0)
+        gelu(3, 1)
+        for m in range(4):
             scatter(m, 0)
             scatter(m, 1)
             store(m)

@@ -1,6 +1,7 @@
 from contextlib import ExitStack
 
 import concourse.mybir as mybir
+from concourse.masks import make_identity
 
 F32 = mybir.dt.float32
 BF16 = mybir.dt.bfloat16
@@ -33,7 +34,7 @@ def tile_list_tabscat_gelu_kernel(tc, tab, w, b, wgo, offs, offs2, out):
         tab32 = tab.bitcast(I32)
 
         planes = keep.tile([P, T], U8, name="planes", align_bytes=64)
-        nc.vector.memset(planes[:].bitcast(I32), 0)
+        nc.gpsimd.memset(planes[:].bitcast(I32), 0)
         wins = []
         for m in range(4):
             win = keep.tile([P, T], F32, name=f"win{m}")
@@ -64,16 +65,23 @@ def tile_list_tabscat_gelu_kernel(tc, tab, w, b, wgo, offs, offs2, out):
             nc.sync.dma_start(out=raws[(a, g)][:], in_=w[512 * a : 512 * (a + 1), c0:c1].rearrange("(p j) c -> p j c", j=4))
 
         nc.sync.dma_start(offs_t[:], offs)
+        bias = keep.tile([P, 4], F32, name="bias")
+        brows = keep.tile([P, P], F32, name="brows")
+        ident = keep.tile([P, P], F32, name="ident")
+        nc.gpsimd.memset(brows[:], 0.0)
+        make_identity(nc, ident[:])
+        nc.scalar.dma_start(out=brows[0:4, :], in_=b.rearrange("(m p) -> m p", p=P))
+        bcols = psum.tile([P, P], F32, name="bcols")
+        nc.tensor.transpose(bcols[:], brows[:], ident[:])
+        nc.scalar.copy(out=bias[:], in_=bcols[:, 0:4])
+        wgo_t = keep.tile([P, S], F32, name="wgo_t")
+        load_tab(0)
+        load_w(0, 0)
         for q in range(4):
             nc.sync.dma_start(
                 out=planes[32 * q : 32 * q + 16, :].bitcast(I32),
                 in_=tab32[:, P * T + T * q : P * T + T * (q + 1)].rearrange("a (r t) -> a r t", r=4),
             )
-        bias = keep.tile([P, 4], F32, name="bias")
-        nc.scalar.dma_start(out=bias[:], in_=b.rearrange("(m p) -> p m", p=P))
-        wgo_t = keep.tile([P, S], F32, name="wgo_t")
-        load_tab(0)
-        load_w(0, 0)
         load_tab(1)
         load_w(1, 0)
         load_tab(2)
@@ -87,7 +95,6 @@ def tile_list_tabscat_gelu_kernel(tc, tab, w, b, wgo, offs, offs2, out):
                 load_w(a, g)
 
         gscales = keep.tile([P, S], U8, name="gscales", align_bytes=64)
-        nc.vector.tensor_copy(gscales[:], planes[:].indirect(offs_t[:]))
         gwords = []
         for a in range(PASSES):
             gw = keep.tile([P, S], U32, name=f"gw{a}", align_bytes=64)
@@ -139,15 +146,19 @@ def tile_list_tabscat_gelu_kernel(tc, tab, w, b, wgo, offs, offs2, out):
         acts = {}
 
         def gelu(m, h):
-            tag = ("grp2_1", "grp2_2", "act2_1", "act3_1")[m] if h else f"act{m}_0"
-            act = keep.tile([P, HALF], F32, name=f"act{m}_{h}", tag=tag, align_bytes=64)
-            acc = accs[0][h][:] if m == 0 else accs[m][0][:, h * HALF : (h + 1) * HALF]
+            if m < 2:
+                tag = ("grp2_1", "grp2_2")[m] if h else f"act{m}_0"
+                act = keep.tile([P, HALF], F32, name=f"act{m}_{h}", tag=tag, align_bytes=64)
+                acc = accs[0][h][:] if m == 0 else accs[m][0][:, h * HALF : (h + 1) * HALF]
+            else:
+                act = keep.tile([P, S], F32, name=f"act{m}_{h}", align_bytes=64)
+                acc = accs[m][0][:]
             nc.scalar.activation(act[:], acc, GELU, bias=bias[:, m : m + 1])
             acts[(m, h)] = act
 
         def scatter(m, h):
-            cols = slice(h * HALF, (h + 1) * HALF)
-            ocols = slice(h * HALF // 16, (h + 1) * HALF // 16)
+            cols = slice(h * HALF, (h + 1) * HALF if m < 2 else S)
+            ocols = slice(cols.start // 16, cols.stop // 16)
             nc.vector.tensor_tensor(wins[m][:].indirect(offs2_t[:, ocols]), acts[(m, h)][:], wgo_t[:, cols], MULT)
 
         def store(m):
@@ -157,6 +168,8 @@ def tile_list_tabscat_gelu_kernel(tc, tab, w, b, wgo, offs, offs2, out):
             quantise(a, 0)
             if a < PASSES - 1:
                 gather(a, 0, S)
+                if a == 0:
+                    nc.vector.tensor_copy(gscales[:], planes[:].indirect(offs_t[:]))
             else:
                 gather(a, 0, HALF)
                 gather(a, HALF, S)
@@ -170,10 +183,9 @@ def tile_list_tabscat_gelu_kernel(tc, tab, w, b, wgo, offs, offs2, out):
                 if a == 2:
                     gelu(g - 1, 1)
             gelu(g, 0)
-        gelu(2, 1)
         gelu(3, 0)
-        gelu(3, 1)
         for m in range(4):
             scatter(m, 0)
-            scatter(m, 1)
+            if m < 2:
+                scatter(m, 1)
             store(m)

from contextlib import ExitStack

import concourse.mybir as mybir
from concourse.masks import make_identity

F32 = mybir.dt.float32
BF16 = mybir.dt.bfloat16
I32 = mybir.dt.int32
U32 = mybir.dt.uint32
U16 = mybir.dt.uint16
U8 = mybir.dt.uint8
FP8X4 = mybir.dt.float8_e4m3fn_x4
MULT = mybir.AluOpType.mult
GELU = mybir.ActivationFunctionType.Gelu_apprx_tanh

K, M, T, S = 2048, 512, 1024, 512
P = 128
PASSES = K // 512
FLOPS = 2 * K * M * S
BYTES = 528 * S * PASSES + 4 * K * M + 4 * M + 4 * S + 4 * P * S // 16 + 4 * M * T

GROUPS = ((0, 128), (128, 256), (256, 512))
HALF = S // 2


def tile_list_tabscat_gelu_kernel(tc, tab, w, b, wgo, offs, offs2, out):
    nc = tc.nc
    with ExitStack() as ctx:
        keep = ctx.enter_context(tc.tile_pool(name="keep", bufs=1))
        psum = ctx.enter_context(tc.psum_pool(name="psum", bufs=1))

        offs_t = keep.tile([P, S // 16], U16, name="offs_t")
        offs2_t = keep.tile([P, S // 16], U16, name="offs2_t")
        tab32 = tab.bitcast(I32)

        planes = keep.tile([P, T], U8, name="planes", align_bytes=64)
        nc.gpsimd.memset(planes[:].bitcast(I32), 0)
        wins = []
        for m in range(4):
            win = keep.tile([P, T], F32, name=f"win{m}")
            wins.append(win)
        nc.vector.memset(wins[0][:], 0.0)
        nc.vector.memset(wins[1][:], 0.0)
        nc.gpsimd.memset(wins[2][:], 0.0)
        nc.gpsimd.memset(wins[3][:], 0.0)
        warm = keep.tile([P, 1], F32, name="warm")
        warm2 = keep.tile([P, 1], F32, name="warm2")
        nc.gpsimd.memset(warm[:], 0.0)
        nc.scalar.activation(warm2[:], warm[:], GELU)

        words = []
        raws = {}
        for a in range(PASSES):
            tw = keep.tile([P, T], I32, name=f"tab{a}", align_bytes=64)
            words.append(tw)
            for g, (c0, c1) in enumerate(GROUPS):
                rw = keep.tile([P, 4, c1 - c0], F32, name=f"raw{a}_{g}")
                raws[(a, g)] = rw

        def load_tab(a):
            nc.sync.dma_start(out=words[a][:], in_=tab32[a, 0 : P * T].rearrange("(p t) -> p t", t=T))

        def load_w(a, g):
            c0, c1 = GROUPS[g]
            nc.sync.dma_start(out=raws[(a, g)][:], in_=w[512 * a : 512 * (a + 1), c0:c1].rearrange("(p j) c -> p j c", j=4))

        nc.sync.dma_start(offs_t[:], offs)
        bias = keep.tile([P, 4], F32, name="bias")
        brows = keep.tile([P, P], F32, name="brows")
        ident = keep.tile([P, P], F32, name="ident")
        nc.gpsimd.memset(brows[:], 0.0)
        make_identity(nc, ident[:])
        nc.scalar.dma_start(out=brows[0:4, :], in_=b.rearrange("(m p) -> m p", p=P))
        bcols = psum.tile([P, P], F32, name="bcols")
        nc.tensor.transpose(bcols[:], brows[:], ident[:])
        nc.scalar.copy(out=bias[:], in_=bcols[:, 0:4])
        wgo_t = keep.tile([P, S], F32, name="wgo_t")
        load_tab(0)
        load_w(0, 0)
        for q in range(4):
            nc.sync.dma_start(
                out=planes[32 * q : 32 * q + 16, :].bitcast(I32),
                in_=tab32[:, P * T + T * q : P * T + T * (q + 1)].rearrange("a (r t) -> a r t", r=4),
            )
        load_tab(1)
        load_w(1, 0)
        load_tab(2)
        load_w(2, 0)
        load_w(3, 0)
        load_tab(3)
        nc.sync.dma_start(offs2_t[:], offs2)
        nc.sync.dma_start(out=wgo_t[:], in_=wgo)
        for g in range(1, len(GROUPS)):
            for a in range(PASSES):
                load_w(a, g)

        gscales = keep.tile([P, S], U8, name="gscales", align_bytes=64)
        gwords = []
        for a in range(PASSES):
            gw = keep.tile([P, S], U32, name=f"gw{a}", align_bytes=64)
            gwords.append(gw)

        accs = []
        for m in range(4):
            row = []
            for h in range(2 if m == 0 else 1):
                acc = psum.tile([P, HALF if m == 0 else S], F32, name=f"acc{m}_{h}")
                row.append(acc)
            accs.append(row)

        codes = {}
        scales = {}

        def quantise(a, g):
            c0, c1 = GROUPS[g]
            width = c1 - c0
            grouped = keep.tile([P, width, 4], BF16, name=f"grp{a}_{g}", tag=f"grp{a}_{g}", align_bytes=64)
            nc.scalar.copy(
                out=grouped[:].rearrange("p (c i) j -> p c j i", i=4),
                in_=raws[(a, g)][:].rearrange("p j (c i) -> p c j i", i=4),
            )
            cd = keep.tile([P, width], U32, name=f"cd{a}_{g}", align_bytes=64)
            sc = keep.tile([P, width], U8, name=f"sc{a}_{g}", align_bytes=64)
            nc.vector.quantize_mx(out=cd[:].bitcast(FP8X4), scales=sc[:], in_=grouped[:].rearrange("p c j -> p (c j)"))
            codes[(a, g)] = cd
            scales[(a, g)] = sc

        def gather(a, h0, h1):
            nc.vector.tensor_copy(gwords[a][:, h0:h1], words[a][:].bitcast(U32).indirect(offs_t[:, h0 // 16 : h1 // 16]))

        def multiply(a, g, h):
            c0, c1 = GROUPS[g]
            for m in range(c0 // P, c1 // P):
                cols = slice(m * P - c0, (m + 1) * P - c0)
                toks = slice(h * HALF, (h + 1) * HALF) if m == 0 else slice(0, S)
                nc.tensor.matmul_mx(
                    out=accs[m][h][:],
                    lhsT=codes[(a, g)][:, cols].bitcast(FP8X4),
                    lhsT_scale=scales[(a, g)][:, cols],
                    rhs=gwords[a][:, toks].bitcast(FP8X4),
                    rhs_scale=gscales[4 * a : P, toks],
                    start=(a == 0),
                    stop=(a == PASSES - 1),
                )

        acts = {}

        def gelu(m, h):
            if m < 2:
                tag = ("grp2_1", "grp2_2")[m] if h else f"act{m}_0"
                act = keep.tile([P, HALF], F32, name=f"act{m}_{h}", tag=tag, align_bytes=64)
                acc = accs[0][h][:] if m == 0 else accs[m][0][:, h * HALF : (h + 1) * HALF]
            else:
                act = keep.tile([P, S], F32, name=f"act{m}_{h}", align_bytes=64)
                acc = accs[m][0][:]
            nc.scalar.activation(act[:], acc, GELU, bias=bias[:, m : m + 1])
            acts[(m, h)] = act

        def scatter(m, h):
            cols = slice(h * HALF, (h + 1) * HALF if m < 2 else S)
            ocols = slice(cols.start // 16, cols.stop // 16)
            nc.vector.tensor_tensor(wins[m][:].indirect(offs2_t[:, ocols]), acts[(m, h)][:], wgo_t[:, cols], MULT)

        def store(m):
            nc.sync.dma_start(out=out[m * P : (m + 1) * P, :], in_=wins[m][:])

        for a in range(PASSES):
            quantise(a, 0)
            if a < PASSES - 1:
                gather(a, 0, S)
                if a == 0:
                    nc.vector.tensor_copy(gscales[:], planes[:].indirect(offs_t[:]))
            else:
                gather(a, 0, HALF)
                gather(a, HALF, S)
            multiply(a, 0, 0)
            multiply(a, 0, 1)
        gelu(0, 0)
        for g in range(1, len(GROUPS)):
            for a in range(PASSES):
                quantise(a, g)
                multiply(a, g, 0)
                if a == 2:
                    gelu(g - 1, 1)
            gelu(g, 0)
        gelu(3, 0)
        for m in range(4):
            scatter(m, 0)
            if m < 2:
                scatter(m, 1)
            store(m)
